import numpy as np
import ml_dtypes


def mxq(x, axis, fmt="e4m3"):
    dtype, down = {"e4m3": (ml_dtypes.float8_e4m3fn, 7), "e5m2": (ml_dtypes.float8_e5m2, 14)}[fmt]
    v = np.moveaxis(np.asarray(x, np.float32).astype(ml_dtypes.bfloat16).astype(np.float64), axis, -1)
    blocks = v.reshape(v.shape[:-1] + (-1, 32))
    amax = np.abs(blocks).max(-1, keepdims=True)
    byte = np.maximum(np.where(amax > 0, np.frexp(amax)[1] - 1 + 127, 0) - down, 1)
    scale = np.exp2(byte - 127.0)
    codes = (blocks / scale).astype(np.float32).astype(dtype).astype(np.float64)
    return np.moveaxis((codes * scale).reshape(v.shape), -1, axis)


WIDE = False


def mx_kscale(k):
    if not WIDE:
        return np.ones(k)
    levels = np.array([10, -10, 5, -5, 0])
    if k % 512:
        return np.exp2(np.random.permutation(np.resize(levels, k // 32))).repeat(32)
    a = np.empty((k // 512, 16))
    for p in range(k // 512):
        a[p, :8] = np.random.permutation(np.resize(levels, 8))
        for g in range(8):
            far = levels[np.abs(levels - a[p, g]) >= 10]
            a[p, g + 8] = far[np.random.randint(len(far))]
    return np.exp2(a.ravel()).repeat(32)


def f64(x):
    return np.asarray(x).astype(np.float64)


def striped(idx):
    return np.tile(idx.reshape(-1, 16).T, (8, 1)).astype(np.uint16)


def unstriped(offs):
    return offs[:16].T.reshape(-1).astype(np.int64)


def striped8(idx):
    return np.concatenate([x.reshape(-1, 16).T for x in idx]).astype(np.uint16)


def runs(offs, k):
    lists = np.stack([offs[16 * r : 16 * r + 16].T.reshape(-1) for r in range(8)]).astype(np.int64)
    return lists[np.arange(k) % 512 // 64]


def pack_weight(w):
    k, n = w.shape
    w = f64(np.asarray(w, np.float32).astype(ml_dtypes.bfloat16)).reshape(k // 32, 32, n)
    amax = np.abs(w).max(1)
    byte = np.clip(np.where(amax > 0, np.frexp(amax)[1] - 1 + 127 - 7, 1), 1, 254)
    scaled = (w * np.exp2(127.0 - byte)[:, None, :]).reshape(k, n).astype(np.float32)
    words = np.ascontiguousarray(scaled.reshape(k // 512, 128, 4, n).transpose(0, 1, 3, 2)).astype(ml_dtypes.float8_e4m3fn).view(np.uint8)
    return words, np.ascontiguousarray(byte.astype(np.uint8).reshape(k // 512, 16, n))


def unpack_weight(words, scales):
    g, p, n, _ = words.shape
    vals = np.ascontiguousarray(words).view(ml_dtypes.float8_e4m3fn).astype(np.float64) * np.repeat(np.exp2(scales.astype(np.float64) - 127.0), 8, axis=1)[..., None]
    return vals.transpose(0, 1, 3, 2).reshape(g * 512, n)


E2M1 = np.array([0.0, 0.5, 1.0, 1.5, 2.0, 3.0, 4.0, 6.0, -0.0, -0.5, -1.0, -1.5, -2.0, -3.0, -4.0, -6.0])


def pack_fp4(w):
    k, n = w.shape
    w = f64(np.asarray(w, np.float32).astype(ml_dtypes.bfloat16)).reshape(k // 32, 32, n)
    amax = np.abs(w).max(1)
    mant, ex = np.frexp(amax / 6.0)
    byte = np.clip(np.where(amax > 0, np.where(mant > 0.5, ex, ex - 1) + 127, 1), 1, 254)
    scaled = (w * np.exp2(127.0 - byte)[:, None, :]).reshape(k, n).astype(np.float32)
    c = np.ascontiguousarray(scaled.reshape(k // 512, 128, 4, n).transpose(0, 1, 3, 2)).astype(ml_dtypes.float4_e2m1fn).view(np.uint8) & 0xF
    words = (c[..., 0::2] | (c[..., 1::2] << 4)).reshape(k // 512, 128, 2 * n)
    return np.ascontiguousarray(words), np.ascontiguousarray(byte.astype(np.uint8).reshape(k // 512, 16, n))


def unpack_fp4(words, scales):
    g, _, n = scales.shape
    words = np.ascontiguousarray(words).reshape(g, 128, n, 2)
    nib = np.empty((g, 128, n, 4), np.uint8)
    nib[..., 0::2] = words & 0xF
    nib[..., 1::2] = words >> 4
    vals = E2M1[nib] * np.repeat(np.exp2(scales.astype(np.float64) - 127.0), 8, axis=1)[..., None]
    return vals.transpose(0, 1, 3, 2).reshape(g * 512, n)


def relu(v):
    return np.maximum(v, 0.0)


def sigmoid(v):
    return 1.0 / (1.0 + np.exp(-np.maximum(v, -700.0)))

def planes(y):
    n, m = y.shape
    v = y.astype(np.float32).astype(ml_dtypes.bfloat16).astype(np.float64).reshape(n // 32, 32, m)
    top = np.abs(v).max(1)
    byte = np.clip(np.where(top > 0, np.frexp(top)[1] - 1 + 127 - 7, 1), 1, 254)
    codes = (v * np.exp2(127.0 - byte)[:, None, :]).reshape(n, m).astype(np.float32).astype(ml_dtypes.float8_e4m3fn).view(np.uint8)
    words = codes.reshape(n // 512, 128, 4, m).transpose(0, 1, 3, 2)
    return np.ascontiguousarray(words), np.ascontiguousarray(byte.astype(np.uint8).reshape(n // 512, 16, m))


K, T, S, N, H = 512, 2048, 512, 512, 512


def setup_inputs():
    n = np.random.standard_normal
    s = mx_kscale(K)[:, None]
    u = mx_kscale(H)
    packed_xT = pack_weight(n((K, T)) * s)
    packed_w1 = pack_fp4(n((K, H)) / np.sqrt(K) / s)
    packed_w2 = pack_fp4(n((H, N)) / np.sqrt(H) / u[:, None])
    return {
        "x_words": packed_xT[0],
        "x_scales": packed_xT[1],
        "w1_words": packed_w1[0],
        "w1_scales": packed_w1[1],
        "gn": (np.random.uniform(0.5, 1.5, (H, 1)) * u[:, None]).astype(np.float32),
        "w2_words": packed_w2[0],
        "w2_scales": packed_w2[1],
        "offs": striped(np.random.permutation(T)[:S]),
        "n1": striped8(np.stack([np.random.permutation(S) for _ in range(8)])),
        "n2": striped8(np.stack([np.random.permutation(S) for _ in range(8)])),
        "n3": striped8(np.stack([np.random.permutation(S) for _ in range(8)])),
        "n4": striped8(np.stack([np.random.permutation(S) for _ in range(8)])),
    }


def reference(x_words, x_scales, w1_words, w1_scales, gn, w2_words, w2_scales, offs, n1, n2, n3, n4):
    xq = unpack_weight(x_words, x_scales)[:, unstriped(offs)]
    y = unpack_fp4(w1_words, w1_scales).T @ xq
    pa = y - (y[np.arange(H)[:, None], runs(n1, H)])
    pb = y[np.arange(H)[:, None], runs(n2, H)] - y
    z = f64(gn) * (relu(np.minimum(pa, pb)) - (relu(-1.0 * np.maximum(pa, pb))))
    h = unpack_fp4(w2_words, w2_scales).T @ mxq(z, 0, "e4m3")
    out_0 = h * (sigmoid(y[np.arange(H)[:, None], runs(n4, H)])) - (0.5 * (h[np.arange(N)[:, None], runs(n3, N)]))
    return (out_0,) + planes(out_0)

@@ -1,0 +1,190 @@
+from contextlib import ExitStack
+
+import concourse.mybir as mybir
+
+F32 = mybir.dt.float32
+BF16 = mybir.dt.bfloat16
+I32 = mybir.dt.int32
+U32 = mybir.dt.uint32
+U16 = mybir.dt.uint16
+U8 = mybir.dt.uint8
+FP8X4 = mybir.dt.float8_e4m3fn_x4
+FP4X4 = mybir.dt.float4_e2m1fn_x4
+ALU = mybir.AluOpType
+ACT = mybir.ActivationFunctionType
+
+P = 128
+PACK = 4
+T = 2048
+S = 512
+HALF = S // 2
+SLICES = ((0, 256), (256, 128), (384, 128))
+FLOPS = 2 * 2 * 512 * 512 * 512
+
+
+def tile_picked_skipgatebminmod_none_po_kernel(
+    tc, x_words, x_scales, w1_words, w1_scales, gn, w2_words, w2_scales, offs, n1, n2, n3, n4, out_0, out_1, out_2
+):
+    nc = tc.nc
+    with ExitStack() as ctx:
+        lists = ctx.enter_context(tc.tile_pool(name="lists", bufs=1))
+        keep = ctx.enter_context(tc.tile_pool(name="keep", bufs=1))
+        psum = ctx.enter_context(tc.psum_pool(name="psum", bufs=1))
+
+        def load_list(src, name):
+            tile = lists.tile([P, S // 16], U16, name=name)
+            nc.sync.dma_start(tile[:], src)
+            return tile
+
+        def load_scale_rows(queues, tile, src):
+            for q in range(4):
+                queues[q].dma_start(tile[32 * q : 32 * q + 4, :].bitcast(I32), src[0, 4 * q : 4 * q + 4, :].bitcast(I32))
+
+        def deal(words_raw, scales_raw, name):
+            words = keep.tile([P, PACK * P * 2], U8, name=name + "_words", tag="dealt_words", align_bytes=64)
+            scales = keep.tile([P, PACK * P], U8, name=name + "_scales", tag="dealt_scales", align_bytes=64)
+            nc.vector.tensor_copy(
+                words[:].rearrange("p (t m b) -> p t m b", t=PACK, b=2),
+                words_raw[:].rearrange("p (m t b) -> p t m b", t=PACK, b=2),
+            )
+            nc.vector.tensor_copy(
+                scales[:].rearrange("p (t m) -> p t m", t=PACK),
+                scales_raw[:].rearrange("p (m t) -> p t m", t=PACK),
+            )
+            return words, scales
+
+        def product(out, w_words, w_scales, t, codes, scales):
+            nc.tensor.matmul_mx(
+                out,
+                lhsT=w_words[:, 2 * P * t : 2 * P * (t + 1)].bitcast(FP4X4),
+                lhsT_scale=w_scales[:, P * t : P * (t + 1)],
+                rhs=codes.bitcast(FP8X4),
+                rhs_scale=scales,
+                start=True,
+                stop=True,
+            )
+
+        def picked(window, offsets, c0, width):
+            return window[:].indirect(offsets[:, c0 // 16 : (c0 + width) // 16])
+
+        def interleave(copy, dst, src):
+            copy(dst[:].rearrange("p (c i) t -> p c t i", i=4), src[:].rearrange("p t (c i) -> p c t i", i=4))
+
+        xs_raw = keep.tile([P, T], U8, name="xs_raw")
+        w1s_raw = keep.tile([P, S], U8, name="w1s_raw")
+        w2s_raw = keep.tile([P, S], U8, name="w2s_raw")
+        warm = keep.tile([P, 1], F32, name="warm")
+        nc.gpsimd.memset(w1s_raw[:].bitcast(I32), 0)
+        nc.vector.memset(xs_raw[:].bitcast(I32), 0)
+        nc.vector.memset(w2s_raw[:].bitcast(I32), 0)
+        nc.vector.memset(warm[:], 0.0)
+
+        offs_t = load_list(offs, "offs_t")
+        w1w_raw = keep.tile([P, 2 * S], U8, name="w1w_raw")
+        nc.sync.dma_start(w1w_raw[:].bitcast(I32), w1_words[0].bitcast(I32))
+        xw_raw = keep.tile([P, T], U32, name="xw_raw")
+        nc.sync.dma_start(xw_raw[:].bitcast(I32), x_words[0].rearrange("p n t -> p (n t)").bitcast(I32))
+        load_scale_rows([nc.scalar] * 4, xs_raw, x_scales)
+        load_scale_rows([nc.gpsimd, nc.scalar, nc.scalar, nc.scalar], w1s_raw, w1_scales)
+        gain = keep.tile([P, PACK], F32, name="gain")
+        nc.gpsimd.dma_start(gain[:], gn.rearrange("(p t) o -> p (t o)", t=PACK))
+        w2w_raw = keep.tile([P, 2 * S], U8, name="w2w_raw")
+        nc.gpsimd.dma_start(w2w_raw[:].bitcast(I32), w2_words[0].bitcast(I32))
+        n1_t = load_list(n1, "n1_t")
+        n2_t = load_list(n2, "n2_t")
+        load_scale_rows([nc.sync] * 4, w2s_raw, w2_scales)
+        n4_t = load_list(n4, "n4_t")
+        n3_t = load_list(n3, "n3_t")
+
+        warm_out = keep.tile([P, 1], F32, name="warm_out")
+        nc.scalar.activation(warm_out[:], warm[:], ACT.Sigmoid)
+
+        neg_gain = keep.tile([P, PACK], F32, name="neg_gain")
+        nc.scalar.activation(neg_gain[:], gain[:], ACT.Copy, scale=-1.0)
+
+        w1_w, w1_s = deal(w1w_raw, w1s_raw, "w1")
+        xs = keep.tile([P, S], U8, name="xs", align_bytes=64)
+        nc.vector.tensor_copy(xs[:], xs_raw[:].indirect(offs_t[:]))
+
+        pos = [keep.tile([P, S], F32, name=f"pos{t}") for t in range(PACK)]
+        neg = [keep.tile([P, S], F32, name=f"neg{t}") for t in range(PACK)]
+        y_sb = [keep.tile([P, S], F32, name=f"y{t}") for t in range(PACK)]
+        half_h = [keep.tile([P, S], F32, name=f"half_h{t}") for t in range(PACK)]
+
+        y_ps = {}
+        for hf in range(2):
+            xw = keep.tile([P, HALF], U32, name=f"xw{hf}", align_bytes=64)
+            nc.vector.tensor_copy(xw[:], picked(xw_raw, offs_t, hf * HALF, HALF))
+            for pair in range(2):
+                bank = psum.tile([P, 2, HALF], F32, name=f"y_bank{hf}{pair}")
+                for u in range(2):
+                    t = 2 * pair + u
+                    product(bank[:, u, :], w1_w, w1_s, t, xw[:], xs[:, hf * HALF : (hf + 1) * HALF])
+                    y_ps[hf, t] = bank[:, u, :]
+        for t in range(PACK):
+            for hf in range(2):
+                cols = slice(hf * HALF, (hf + 1) * HALF)
+                nc.scalar.activation(pos[t][:, cols], y_ps[hf, t], ACT.Copy, scale=gain[:, t : t + 1])
+                nc.scalar.activation(neg[t][:, cols], y_ps[hf, t], ACT.Copy, scale=neg_gain[:, t : t + 1])
+        w2_w, w2_s = deal(w2w_raw, w2s_raw, "w2")
+        for t in range(PACK):
+            for hf in range(2):
+                nc.scalar.copy(y_sb[t][:, hf * HALF : (hf + 1) * HALF], y_ps[hf, t])
+
+        gated = []
+        for s, (c0, width) in enumerate(SLICES):
+            cols = slice(c0, c0 + width)
+            last = s == len(SLICES) - 1
+            pa = keep.tile([P, PACK, width], F32, name=f"pa{s}")
+            pb = keep.tile([P, PACK, width], F32, name=f"pb{s}")
+            for t in range(PACK):
+                nc.vector.tensor_tensor(pa[:, t, :], picked(neg[t], n1_t, c0, width), pos[t][:, cols], ALU.add)
+                nc.vector.tensor_tensor(pb[:, t, :], picked(pos[t], n2_t, c0, width), neg[t][:, cols], ALU.add)
+            floor = keep.tile([P, PACK, width], F32, name=f"floor{s}")
+            z = keep.tile([P, PACK, width], F32, name=f"z{s}")
+            for pair in range(2):
+                rows = slice(2 * pair, 2 * pair + 2)
+                nc.vector.scalar_tensor_tensor(floor[:, rows, :], pb[:, rows, :], 0.0, pa[:, rows, :], ALU.min, ALU.max)
+            for pair in range(2):
+                rows = slice(2 * pair, 2 * pair + 2)
+                nc.vector.scalar_tensor_tensor(z[:, rows, :], pb[:, rows, :], 0.0, floor[:, rows, :], ALU.max, ALU.min)
+            z_bf = keep.tile([P, width, PACK], BF16, name=f"z_bf{s}", align_bytes=64)
+            interleave(nc.vector.tensor_copy if last else nc.scalar.copy, z_bf, z)
+            z_codes = keep.tile([P, width], U32, name=f"z_codes{s}", align_bytes=64)
+            z_scales = keep.tile([P, width], U8, name=f"z_scales{s}", align_bytes=64)
+            nc.vector.quantize_mx(z_codes[:].bitcast(FP8X4), z_scales[:], z_bf[:].rearrange("p c t -> p (c t)"))
+
+            gate = keep.tile([P, PACK, width], F32, name=f"gate{s}")
+            for t in range(PACK):
+                nc.scalar.activation(gate[:, t, :], picked(y_sb[t], n4_t, c0, width), ACT.Sigmoid)
+
+            product_s = keep.tile([P, PACK, width], F32, name=f"gated{s}")
+            per_bank = S // width
+            for b in range(PACK // per_bank):
+                bank = psum.tile([P, per_bank, width], F32, name=f"h_bank{s}{b}")
+                for u in range(per_bank):
+                    product(bank[:, u, :], w2_w, w2_s, b * per_bank + u, z_codes[:], z_scales[:])
+                for u in range(per_bank):
+                    nc.scalar.activation(half_h[b * per_bank + u][:, cols], bank[:, u, :], ACT.Copy, scale=-0.5)
+                rows = slice(b * per_bank, (b + 1) * per_bank)
+                nc.vector.tensor_tensor(product_s[:, rows, :], bank[:], gate[:, rows, :], ALU.mult)
+            gated.append(product_s)
+
+        out_rows = out_0.rearrange("(p t) s -> p t s", t=PACK)
+        out_words = out_1[0].rearrange("p n t -> p (n t)").bitcast(I32)
+        o_scales = keep.tile([P, S], U8, name="o_scales", align_bytes=64)
+        for s, (c0, width) in enumerate(SLICES):
+            cols = slice(c0, c0 + width)
+            last = s == len(SLICES) - 1
+            res = keep.tile([P, PACK, width], F32, name=f"res{s}")
+            for t in range(PACK):
+                nc.vector.tensor_tensor(res[:, t, :], picked(half_h[t], n3_t, c0, width), gated[s][:, t, :], ALU.add)
+            nc.sync.dma_start(out_rows[:, :, cols], res[:])
+            o_bf = keep.tile([P, width, PACK], BF16, name=f"o_bf{s}", align_bytes=64)
+            interleave(nc.vector.tensor_copy if last else nc.scalar.copy, o_bf, res)
+            o_codes = keep.tile([P, width], U32, name=f"o_codes{s}", align_bytes=64)
+            nc.vector.quantize_mx(o_codes[:].bitcast(FP8X4), o_scales[:, cols], o_bf[:].rearrange("p c t -> p (c t)"))
+            nc.sync.dma_start(out_words[:, cols], o_codes[:].bitcast(I32))
+        for q in range(4):
+            queue = nc.scalar if q % 2 == 0 else nc.sync
+            queue.dma_start(out_2[0, 4 * q : 4 * q + 4, :].bitcast(I32), o_scales[32 * q : 32 * q + 4, :].bitcast(I32))

@@ -40,18 +40,21 @@ def tile_picked_skipgatebminmod_none_po_kernel(
             for q in range(4):
                 queues[q].dma_start(tile[32 * q : 32 * q + 4, :].bitcast(I32), src[0, 4 * q : 4 * q + 4, :].bitcast(I32))
 
-        def deal(words_raw, scales_raw, name):
-            words = keep.tile([P, PACK * P * 2], U8, name=name + "_words", tag="dealt_words", align_bytes=64)
-            scales = keep.tile([P, PACK * P], U8, name=name + "_scales", tag="dealt_scales", align_bytes=64)
+        def deal_words(raw, name):
+            words = keep.tile([P, PACK * P * 2], U8, name=name, tag="dealt_words", align_bytes=64)
             nc.vector.tensor_copy(
                 words[:].rearrange("p (t m b) -> p t m b", t=PACK, b=2),
-                words_raw[:].rearrange("p (m t b) -> p t m b", t=PACK, b=2),
+                raw[:].rearrange("p (m t b) -> p t m b", t=PACK, b=2),
             )
+            return words
+
+        def deal_scales(raw, name, tag):
+            scales = keep.tile([P, PACK * P], U8, name=name, tag=tag, align_bytes=64)
             nc.vector.tensor_copy(
                 scales[:].rearrange("p (t m) -> p t m", t=PACK),
-                scales_raw[:].rearrange("p (m t) -> p t m", t=PACK),
+                raw[:].rearrange("p (m t) -> p t m", t=PACK),
             )
-            return words, scales
+            return scales
 
         def product(out, w_words, w_scales, t, codes, scales):
             nc.tensor.matmul_mx(
@@ -68,7 +71,7 @@ def tile_picked_skipgatebminmod_none_po_kernel(
             return window[:].indirect(offsets[:, c0 // 16 : (c0 + width) // 16])
 
         def interleave(copy, dst, src):
-            copy(dst[:].rearrange("p (c i) t -> p c t i", i=4), src[:].rearrange("p t (c i) -> p c t i", i=4))
+            copy(dst.rearrange("p (c i) t -> p c t i", i=4), src.rearrange("p t (c i) -> p c t i", i=4))
 
         xs_raw = keep.tile([P, T], U8, name="xs_raw")
         w1s_raw = keep.tile([P, S], U8, name="w1s_raw")
@@ -81,7 +84,11 @@ def tile_picked_skipgatebminmod_none_po_kernel(
 
         offs_t = load_list(offs, "offs_t")
         w1w_raw = keep.tile([P, 2 * S], U8, name="w1w_raw")
-        nc.sync.dma_start(w1w_raw[:].bitcast(I32), w1_words[0].bitcast(I32))
+        nc.scalar.dma_start(w1w_raw[:].bitcast(I32), w1_words[0].bitcast(I32))
+        n1_t = load_list(n1, "n1_t")
+        n2_t = load_list(n2, "n2_t")
+        n4_t = load_list(n4, "n4_t")
+        n3_t = load_list(n3, "n3_t")
         xw_raw = keep.tile([P, T], U32, name="xw_raw")
         nc.sync.dma_start(xw_raw[:].bitcast(I32), x_words[0].rearrange("p n t -> p (n t)").bitcast(I32))
         load_scale_rows([nc.scalar] * 4, xs_raw, x_scales)
@@ -90,11 +97,7 @@ def tile_picked_skipgatebminmod_none_po_kernel(
         nc.gpsimd.dma_start(gain[:], gn.rearrange("(p t) o -> p (t o)", t=PACK))
         w2w_raw = keep.tile([P, 2 * S], U8, name="w2w_raw")
         nc.gpsimd.dma_start(w2w_raw[:].bitcast(I32), w2_words[0].bitcast(I32))
-        n1_t = load_list(n1, "n1_t")
-        n2_t = load_list(n2, "n2_t")
         load_scale_rows([nc.sync] * 4, w2s_raw, w2_scales)
-        n4_t = load_list(n4, "n4_t")
-        n3_t = load_list(n3, "n3_t")
 
         warm_out = keep.tile([P, 1], F32, name="warm_out")
         nc.scalar.activation(warm_out[:], warm[:], ACT.Sigmoid)
@@ -102,9 +105,10 @@ def tile_picked_skipgatebminmod_none_po_kernel(
         neg_gain = keep.tile([P, PACK], F32, name="neg_gain")
         nc.scalar.activation(neg_gain[:], gain[:], ACT.Copy, scale=-1.0)
 
-        w1_w, w1_s = deal(w1w_raw, w1s_raw, "w1")
+        w1_w = deal_words(w1w_raw, "w1_w")
         xs = keep.tile([P, S], U8, name="xs", align_bytes=64)
         nc.vector.tensor_copy(xs[:], xs_raw[:].indirect(offs_t[:]))
+        w1_s = deal_scales(w1s_raw, "w1_s", "w1_s")
 
         pos = [keep.tile([P, S], F32, name=f"pos{t}") for t in range(PACK)]
         neg = [keep.tile([P, S], F32, name=f"neg{t}") for t in range(PACK)]
@@ -126,49 +130,86 @@ def tile_picked_skipgatebminmod_none_po_kernel(
                 cols = slice(hf * HALF, (hf + 1) * HALF)
                 nc.scalar.activation(pos[t][:, cols], y_ps[hf, t], ACT.Copy, scale=gain[:, t : t + 1])
                 nc.scalar.activation(neg[t][:, cols], y_ps[hf, t], ACT.Copy, scale=neg_gain[:, t : t + 1])
-        w2_w, w2_s = deal(w2w_raw, w2s_raw, "w2")
+        w2_w = deal_words(w2w_raw, "w2_w")
         for t in range(PACK):
             for hf in range(2):
                 nc.scalar.copy(y_sb[t][:, hf * HALF : (hf + 1) * HALF], y_ps[hf, t])
 
-        gated = []
-        for s, (c0, width) in enumerate(SLICES):
-            cols = slice(c0, c0 + width)
-            last = s == len(SLICES) - 1
-            pa = keep.tile([P, PACK, width], F32, name=f"pa{s}")
-            pb = keep.tile([P, PACK, width], F32, name=f"pb{s}")
+        def look_up_differences(hf):
+            c0 = hf * HALF
+            cols = slice(c0, c0 + HALF)
+            pa = keep.tile([P, PACK, HALF], F32, name=f"pa{hf}", tag="pa", align_bytes=64)
+            pb = keep.tile([P, PACK, HALF], F32, name=f"pb{hf}", tag="pb", align_bytes=64)
             for t in range(PACK):
-                nc.vector.tensor_tensor(pa[:, t, :], picked(neg[t], n1_t, c0, width), pos[t][:, cols], ALU.add)
-                nc.vector.tensor_tensor(pb[:, t, :], picked(pos[t], n2_t, c0, width), neg[t][:, cols], ALU.add)
-            floor = keep.tile([P, PACK, width], F32, name=f"floor{s}")
-            z = keep.tile([P, PACK, width], F32, name=f"z{s}")
-            for pair in range(2):
-                rows = slice(2 * pair, 2 * pair + 2)
-                nc.vector.scalar_tensor_tensor(floor[:, rows, :], pb[:, rows, :], 0.0, pa[:, rows, :], ALU.min, ALU.max)
-            for pair in range(2):
-                rows = slice(2 * pair, 2 * pair + 2)
-                nc.vector.scalar_tensor_tensor(z[:, rows, :], pb[:, rows, :], 0.0, floor[:, rows, :], ALU.max, ALU.min)
-            z_bf = keep.tile([P, width, PACK], BF16, name=f"z_bf{s}", align_bytes=64)
-            interleave(nc.vector.tensor_copy if last else nc.scalar.copy, z_bf, z)
+                nc.vector.tensor_tensor(pa[:, t, :], picked(neg[t], n1_t, c0, HALF), pos[t][:, cols], ALU.add)
+                nc.vector.tensor_tensor(pb[:, t, :], picked(pos[t], n2_t, c0, HALF), neg[t][:, cols], ALU.add)
+            return pa, pb
+
+        def minmod(hf, pa, pb, parts):
+            floor = keep.tile([P, PACK, HALF], F32, name=f"floor{hf}", tag=f"staged{hf}", align_bytes=64)
+            z = keep.tile([P, PACK, HALF], F32, name=f"z{hf}")
+            for part in parts:
+                nc.vector.scalar_tensor_tensor(floor[part], pb[part], 0.0, pa[part], ALU.min, ALU.max)
+            for part in parts:
+                nc.vector.scalar_tensor_tensor(z[part], pb[part], 0.0, floor[part], ALU.max, ALU.min)
+            return z
+
+        def look_up_gate(hf):
+            gate = keep.tile([P, PACK, HALF], F32, name=f"gate{hf}")
+            for t in range(PACK):
+                nc.scalar.activation(gate[:, t, :], picked(y_sb[t], n4_t, hf * HALF, HALF), ACT.Sigmoid)
+            return gate
+
+        def round_z(s, z, copy, tag):
+            c0, width = SLICES[s]
+            z_bf = keep.tile([P, width, PACK], BF16, name=f"z_bf{s}", tag=tag, align_bytes=64)
+            interleave(copy, z_bf[:], z[:, :, c0 % HALF : c0 % HALF + width])
+            return z_bf
+
+        def second_product(s, z_bf):
+            c0, width = SLICES[s]
             z_codes = keep.tile([P, width], U32, name=f"z_codes{s}", align_bytes=64)
             z_scales = keep.tile([P, width], U8, name=f"z_scales{s}", align_bytes=64)
             nc.vector.quantize_mx(z_codes[:].bitcast(FP8X4), z_scales[:], z_bf[:].rearrange("p c t -> p (c t)"))
-
-            gate = keep.tile([P, PACK, width], F32, name=f"gate{s}")
-            for t in range(PACK):
-                nc.scalar.activation(gate[:, t, :], picked(y_sb[t], n4_t, c0, width), ACT.Sigmoid)
-
-            product_s = keep.tile([P, PACK, width], F32, name=f"gated{s}")
             per_bank = S // width
+            banks = []
             for b in range(PACK // per_bank):
                 bank = psum.tile([P, per_bank, width], F32, name=f"h_bank{s}{b}")
                 for u in range(per_bank):
                     product(bank[:, u, :], w2_w, w2_s, b * per_bank + u, z_codes[:], z_scales[:])
                 for u in range(per_bank):
-                    nc.scalar.activation(half_h[b * per_bank + u][:, cols], bank[:, u, :], ACT.Copy, scale=-0.5)
+                    nc.scalar.activation(half_h[b * per_bank + u][:, c0 : c0 + width], bank[:, u, :], ACT.Copy, scale=-0.5)
+                banks.append(bank)
+            return banks
+
+        every = slice(None)
+        by_rows = [(every, slice(0, 2), every), (every, slice(2, 4), every)]
+        by_cols = [(every, every, slice(0, HALF // 2)), (every, every, slice(HALF // 2, HALF))]
+
+        pa, pb = look_up_differences(0)
+        gates = [look_up_gate(0)]
+        z = minmod(0, pa, pb, by_rows)
+        w2_s = deal_scales(w2s_raw, "w2_s", "staged0")
+        z_bf = round_z(0, z, nc.scalar.copy, "staged1")
+        pa, pb = look_up_differences(1)
+        gates.append(look_up_gate(1))
+        h_banks = [second_product(0, z_bf)]
+        z = minmod(1, pa, pb, by_cols)
+        z_bf1 = round_z(1, z, nc.scalar.copy, "z_bf1")
+        z_bf2 = round_z(2, z, nc.vector.tensor_copy, "z_bf2")
+        h_banks.append(second_product(1, z_bf1))
+        h_banks.append(second_product(2, z_bf2))
+
+        gated = []
+        for s, tag in enumerate(("pb", "pa", "gated")):
+            c0, width = SLICES[s]
+            gated_s = keep.tile([P, PACK, width], F32, name=f"gated{s}", tag=tag, align_bytes=64)
+            per_bank = S // width
+            for b, bank in enumerate(h_banks[s]):
                 rows = slice(b * per_bank, (b + 1) * per_bank)
-                nc.vector.tensor_tensor(product_s[:, rows, :], bank[:], gate[:, rows, :], ALU.mult)
-            gated.append(product_s)
+                gate = gates[c0 // HALF][:, rows, c0 % HALF : c0 % HALF + width]
+                nc.vector.tensor_tensor(gated_s[:, rows, :], bank[:], gate, ALU.mult)
+            gated.append(gated_s)
 
         out_rows = out_0.rearrange("(p t) s -> p t s", t=PACK)
         out_words = out_1[0].rearrange("p n t -> p (n t)").bitcast(I32)
@@ -181,7 +222,7 @@ def tile_picked_skipgatebminmod_none_po_kernel(
                 nc.vector.tensor_tensor(res[:, t, :], picked(half_h[t], n3_t, c0, width), gated[s][:, t, :], ALU.add)
             nc.sync.dma_start(out_rows[:, :, cols], res[:])
             o_bf = keep.tile([P, width, PACK], BF16, name=f"o_bf{s}", align_bytes=64)
-            interleave(nc.vector.tensor_copy if last else nc.scalar.copy, o_bf, res)
+            interleave(nc.vector.tensor_copy if last else nc.scalar.copy, o_bf[:], res[:])
             o_codes = keep.tile([P, width], U32, name=f"o_codes{s}", align_bytes=64)
             nc.vector.quantize_mx(o_codes[:].bitcast(FP8X4), o_scales[:, cols], o_bf[:].rearrange("p c t -> p (c t)"))
             nc.sync.dma_start(out_words[:, cols], o_codes[:].bitcast(I32))

@@ -41,7 +41,7 @@ def tile_picked_skipgatebminmod_none_po_kernel(
                 queues[q].dma_start(tile[32 * q : 32 * q + 4, :].bitcast(I32), src[0, 4 * q : 4 * q + 4, :].bitcast(I32))
 
         def deal_words(raw, name):
-            words = keep.tile([P, PACK * P * 2], U8, name=name, tag="dealt_words", align_bytes=64)
+            words = keep.tile([P, PACK * P * 2], U8, name=name, align_bytes=64)
             nc.vector.tensor_copy(
                 words[:].rearrange("p (t m b) -> p t m b", t=PACK, b=2),
                 raw[:].rearrange("p (m t b) -> p t m b", t=PACK, b=2),
@@ -76,31 +76,26 @@ def tile_picked_skipgatebminmod_none_po_kernel(
         xs_raw = keep.tile([P, T], U8, name="xs_raw")
         w1s_raw = keep.tile([P, S], U8, name="w1s_raw")
         w2s_raw = keep.tile([P, S], U8, name="w2s_raw")
-        warm = keep.tile([P, 1], F32, name="warm")
-        nc.gpsimd.memset(w1s_raw[:].bitcast(I32), 0)
-        nc.vector.memset(xs_raw[:].bitcast(I32), 0)
+        nc.gpsimd.memset(xs_raw[:].bitcast(I32), 0)
+        nc.vector.memset(w1s_raw[:].bitcast(I32), 0)
         nc.vector.memset(w2s_raw[:].bitcast(I32), 0)
-        nc.vector.memset(warm[:], 0.0)
 
         offs_t = load_list(offs, "offs_t")
+        gain = keep.tile([P, PACK], F32, name="gain")
+        nc.sync.dma_start(gain[:], gn.rearrange("(p t) o -> p (t o)", t=PACK))
         w1w_raw = keep.tile([P, 2 * S], U8, name="w1w_raw")
-        nc.scalar.dma_start(w1w_raw[:].bitcast(I32), w1_words[0].bitcast(I32))
+        nc.sync.dma_start(w1w_raw[:].bitcast(I32), w1_words[0].bitcast(I32))
+        load_scale_rows([nc.scalar, nc.scalar, nc.sync, nc.sync], xs_raw, x_scales)
+        xw_raw = keep.tile([P, T], U32, name="xw_raw")
+        nc.sync.dma_start(xw_raw[:].bitcast(I32), x_words[0].rearrange("p n t -> p (n t)").bitcast(I32))
+        load_scale_rows([nc.gpsimd, nc.gpsimd, nc.gpsimd, nc.sync], w1s_raw, w1_scales)
+        w2w_raw = keep.tile([P, 2 * S], U8, name="w2w_raw")
+        nc.sync.dma_start(w2w_raw[:].bitcast(I32), w2_words[0].bitcast(I32))
         n1_t = load_list(n1, "n1_t")
         n2_t = load_list(n2, "n2_t")
         n4_t = load_list(n4, "n4_t")
         n3_t = load_list(n3, "n3_t")
-        xw_raw = keep.tile([P, T], U32, name="xw_raw")
-        nc.sync.dma_start(xw_raw[:].bitcast(I32), x_words[0].rearrange("p n t -> p (n t)").bitcast(I32))
-        load_scale_rows([nc.scalar] * 4, xs_raw, x_scales)
-        load_scale_rows([nc.gpsimd, nc.scalar, nc.scalar, nc.scalar], w1s_raw, w1_scales)
-        gain = keep.tile([P, PACK], F32, name="gain")
-        nc.gpsimd.dma_start(gain[:], gn.rearrange("(p t) o -> p (t o)", t=PACK))
-        w2w_raw = keep.tile([P, 2 * S], U8, name="w2w_raw")
-        nc.gpsimd.dma_start(w2w_raw[:].bitcast(I32), w2_words[0].bitcast(I32))
         load_scale_rows([nc.sync] * 4, w2s_raw, w2_scales)
-
-        warm_out = keep.tile([P, 1], F32, name="warm_out")
-        nc.scalar.activation(warm_out[:], warm[:], ACT.Sigmoid)
 
         neg_gain = keep.tile([P, PACK], F32, name="neg_gain")
         nc.scalar.activation(neg_gain[:], gain[:], ACT.Copy, scale=-1.0)
@@ -108,7 +103,6 @@ def tile_picked_skipgatebminmod_none_po_kernel(
         w1_w = deal_words(w1w_raw, "w1_w")
         xs = keep.tile([P, S], U8, name="xs", align_bytes=64)
         nc.vector.tensor_copy(xs[:], xs_raw[:].indirect(offs_t[:]))
-        w1_s = deal_scales(w1s_raw, "w1_s", "w1_s")
 
         pos = [keep.tile([P, S], F32, name=f"pos{t}") for t in range(PACK)]
         neg = [keep.tile([P, S], F32, name=f"neg{t}") for t in range(PACK)]
@@ -119,17 +113,17 @@ def tile_picked_skipgatebminmod_none_po_kernel(
         for hf in range(2):
             xw = keep.tile([P, HALF], U32, name=f"xw{hf}", align_bytes=64)
             nc.vector.tensor_copy(xw[:], picked(xw_raw, offs_t, hf * HALF, HALF))
-            for pair in range(2):
-                bank = psum.tile([P, 2, HALF], F32, name=f"y_bank{hf}{pair}")
-                for u in range(2):
-                    t = 2 * pair + u
-                    product(bank[:, u, :], w1_w, w1_s, t, xw[:], xs[:, hf * HALF : (hf + 1) * HALF])
-                    y_ps[hf, t] = bank[:, u, :]
+            if hf == 0:
+                w1_s = deal_scales(w1s_raw, "w1_s", "w1_s")
+            for t in range(PACK):
+                bank = psum.tile([P, HALF], F32, name=f"y_bank{hf}{t}", tag=f"bank{hf}{t}")
+                product(bank[:], w1_w, w1_s, t, xw[:], xs[:, hf * HALF : (hf + 1) * HALF])
+                y_ps[hf, t] = bank[:]
         for t in range(PACK):
             for hf in range(2):
                 cols = slice(hf * HALF, (hf + 1) * HALF)
-                nc.scalar.activation(pos[t][:, cols], y_ps[hf, t], ACT.Copy, scale=gain[:, t : t + 1])
                 nc.scalar.activation(neg[t][:, cols], y_ps[hf, t], ACT.Copy, scale=neg_gain[:, t : t + 1])
+                nc.scalar.activation(pos[t][:, cols], y_ps[hf, t], ACT.Copy, scale=gain[:, t : t + 1])
         w2_w = deal_words(w2w_raw, "w2_w")
         for t in range(PACK):
             for hf in range(2):
@@ -154,10 +148,11 @@ def tile_picked_skipgatebminmod_none_po_kernel(
                 nc.vector.scalar_tensor_tensor(z[part], pb[part], 0.0, floor[part], ALU.max, ALU.min)
             return z
 
-        def look_up_gate(hf):
-            gate = keep.tile([P, PACK, HALF], F32, name=f"gate{hf}")
+        def look_up_gate(s):
+            c0, width = SLICES[s]
+            gate = keep.tile([P, PACK, width], F32, name=f"gate{s}")
             for t in range(PACK):
-                nc.scalar.activation(gate[:, t, :], picked(y_sb[t], n4_t, hf * HALF, HALF), ACT.Sigmoid)
+                nc.scalar.activation(gate[:, t, :], picked(y_sb[t], n4_t, c0, width), ACT.Sigmoid)
             return gate
 
         def round_z(s, z, copy, tag):
@@ -174,7 +169,7 @@ def tile_picked_skipgatebminmod_none_po_kernel(
             per_bank = S // width
             banks = []
             for b in range(PACK // per_bank):
-                bank = psum.tile([P, per_bank, width], F32, name=f"h_bank{s}{b}")
+                bank = psum.tile([P, per_bank, width], F32, name=f"h_bank{s}{b}", tag=f"bank{min(s, 1)}{b + s // 2}")
                 for u in range(per_bank):
                     product(bank[:, u, :], w2_w, w2_s, b * per_bank + u, z_codes[:], z_scales[:])
                 for u in range(per_bank):
@@ -199,17 +194,18 @@ def tile_picked_skipgatebminmod_none_po_kernel(
         z_bf2 = round_z(2, z, nc.vector.tensor_copy, "z_bf2")
         h_banks.append(second_product(1, z_bf1))
         h_banks.append(second_product(2, z_bf2))
+        gates.append(look_up_gate(2))
 
-        gated = []
-        for s, tag in enumerate(("pb", "pa", "gated")):
+        def gate_h(s, tag):
             c0, width = SLICES[s]
             gated_s = keep.tile([P, PACK, width], F32, name=f"gated{s}", tag=tag, align_bytes=64)
             per_bank = S // width
             for b, bank in enumerate(h_banks[s]):
                 rows = slice(b * per_bank, (b + 1) * per_bank)
-                gate = gates[c0 // HALF][:, rows, c0 % HALF : c0 % HALF + width]
-                nc.vector.tensor_tensor(gated_s[:, rows, :], bank[:], gate, ALU.mult)
-            gated.append(gated_s)
+                nc.vector.tensor_tensor(gated_s[:, rows, :], bank[:], gates[s][:, rows, :], ALU.mult)
+            return gated_s
+
+        gated = [gate_h(0, "pb"), gate_h(1, "pa")]
 
         out_rows = out_0.rearrange("(p t) s -> p t s", t=PACK)
         out_words = out_1[0].rearrange("p n t -> p (n t)").bitcast(I32)
@@ -220,6 +216,8 @@ def tile_picked_skipgatebminmod_none_po_kernel(
             res = keep.tile([P, PACK, width], F32, name=f"res{s}")
             for t in range(PACK):
                 nc.vector.tensor_tensor(res[:, t, :], picked(half_h[t], n3_t, c0, width), gated[s][:, t, :], ALU.add)
+            if s == 0:
+                gated.append(gate_h(2, "gated2"))
             nc.sync.dma_start(out_rows[:, :, cols], res[:])
             o_bf = keep.tile([P, width, PACK], BF16, name=f"o_bf{s}", align_bytes=64)
             interleave(nc.vector.tensor_copy if last else nc.scalar.copy, o_bf[:], res[:])

@@ -36,9 +36,9 @@ def tile_picked_skipgatebminmod_none_po_kernel(
             nc.sync.dma_start(tile[:], src)
             return tile
 
-        def load_scale_rows(queues, tile, src):
-            for q in range(4):
-                queues[q].dma_start(tile[32 * q : 32 * q + 4, :].bitcast(I32), src[0, 4 * q : 4 * q + 4, :].bitcast(I32))
+        def load_scale_rows(tile, src, queues):
+            for q, queue in queues.items():
+                queue.dma_start(tile[32 * q : 32 * q + 4, :].bitcast(I32), src[0, 4 * q : 4 * q + 4, :].bitcast(I32))
 
         def deal_words(raw, name):
             words = keep.tile([P, PACK * P * 2], U8, name=name, align_bytes=64)
@@ -48,8 +48,8 @@ def tile_picked_skipgatebminmod_none_po_kernel(
             )
             return words
 
-        def deal_scales(raw, name, tag):
-            scales = keep.tile([P, PACK * P], U8, name=name, tag=tag, align_bytes=64)
+        def deal_scales(raw, name):
+            scales = keep.tile([P, PACK * P], U8, name=name, align_bytes=64)
             nc.vector.tensor_copy(
                 scales[:].rearrange("p (t m) -> p t m", t=PACK),
                 raw[:].rearrange("p (m t) -> p t m", t=PACK),
@@ -76,26 +76,27 @@ def tile_picked_skipgatebminmod_none_po_kernel(
         xs_raw = keep.tile([P, T], U8, name="xs_raw")
         w1s_raw = keep.tile([P, S], U8, name="w1s_raw")
         w2s_raw = keep.tile([P, S], U8, name="w2s_raw")
-        nc.gpsimd.memset(xs_raw[:].bitcast(I32), 0)
-        nc.vector.memset(w1s_raw[:].bitcast(I32), 0)
+        nc.vector.memset(xs_raw[:].bitcast(I32), 0)
+        nc.gpsimd.memset(w1s_raw[:].bitcast(I32), 0)
         nc.vector.memset(w2s_raw[:].bitcast(I32), 0)
 
         offs_t = load_list(offs, "offs_t")
-        gain = keep.tile([P, PACK], F32, name="gain")
-        nc.sync.dma_start(gain[:], gn.rearrange("(p t) o -> p (t o)", t=PACK))
         w1w_raw = keep.tile([P, 2 * S], U8, name="w1w_raw")
         nc.sync.dma_start(w1w_raw[:].bitcast(I32), w1_words[0].bitcast(I32))
-        load_scale_rows([nc.scalar, nc.scalar, nc.sync, nc.sync], xs_raw, x_scales)
+        load_scale_rows(xs_raw, x_scales, {0: nc.scalar, 1: nc.sync, 2: nc.scalar, 3: nc.sync})
+        load_scale_rows(w1s_raw, w1_scales, {0: nc.gpsimd, 1: nc.gpsimd, 2: nc.scalar})
         xw_raw = keep.tile([P, T], U32, name="xw_raw")
         nc.sync.dma_start(xw_raw[:].bitcast(I32), x_words[0].rearrange("p n t -> p (n t)").bitcast(I32))
-        load_scale_rows([nc.gpsimd, nc.gpsimd, nc.gpsimd, nc.sync], w1s_raw, w1_scales)
+        load_scale_rows(w1s_raw, w1_scales, {3: nc.sync})
+        gain = keep.tile([P, PACK], F32, name="gain")
+        nc.sync.dma_start(gain[:], gn.rearrange("(p t) o -> p (t o)", t=PACK))
         w2w_raw = keep.tile([P, 2 * S], U8, name="w2w_raw")
         nc.sync.dma_start(w2w_raw[:].bitcast(I32), w2_words[0].bitcast(I32))
         n1_t = load_list(n1, "n1_t")
         n2_t = load_list(n2, "n2_t")
+        load_scale_rows(w2s_raw, w2_scales, {0: nc.sync, 1: nc.sync, 2: nc.gpsimd, 3: nc.gpsimd})
         n4_t = load_list(n4, "n4_t")
         n3_t = load_list(n3, "n3_t")
-        load_scale_rows([nc.sync] * 4, w2s_raw, w2_scales)
 
         neg_gain = keep.tile([P, PACK], F32, name="neg_gain")
         nc.scalar.activation(neg_gain[:], gain[:], ACT.Copy, scale=-1.0)
@@ -114,7 +115,7 @@ def tile_picked_skipgatebminmod_none_po_kernel(
             xw = keep.tile([P, HALF], U32, name=f"xw{hf}", align_bytes=64)
             nc.vector.tensor_copy(xw[:], picked(xw_raw, offs_t, hf * HALF, HALF))
             if hf == 0:
-                w1_s = deal_scales(w1s_raw, "w1_s", "w1_s")
+                w1_s = deal_scales(w1s_raw, "w1_s")
             for t in range(PACK):
                 bank = psum.tile([P, HALF], F32, name=f"y_bank{hf}{t}", tag=f"bank{hf}{t}")
                 product(bank[:], w1_w, w1_s, t, xw[:], xs[:, hf * HALF : (hf + 1) * HALF])
@@ -125,6 +126,7 @@ def tile_picked_skipgatebminmod_none_po_kernel(
                 nc.scalar.activation(neg[t][:, cols], y_ps[hf, t], ACT.Copy, scale=neg_gain[:, t : t + 1])
                 nc.scalar.activation(pos[t][:, cols], y_ps[hf, t], ACT.Copy, scale=gain[:, t : t + 1])
         w2_w = deal_words(w2w_raw, "w2_w")
+        w2_s = deal_scales(w2s_raw, "w2_s")
         for t in range(PACK):
             for hf in range(2):
                 nc.scalar.copy(y_sb[t][:, hf * HALF : (hf + 1) * HALF], y_ps[hf, t])
@@ -184,7 +186,6 @@ def tile_picked_skipgatebminmod_none_po_kernel(
         pa, pb = look_up_differences(0)
         gates = [look_up_gate(0)]
         z = minmod(0, pa, pb, by_rows)
-        w2_s = deal_scales(w2s_raw, "w2_s", "staged0")
         z_bf = round_z(0, z, nc.scalar.copy, "staged1")
         pa, pb = look_up_differences(1)
         gates.append(look_up_gate(1))

from contextlib import ExitStack

import concourse.mybir as mybir

F32 = mybir.dt.float32
BF16 = mybir.dt.bfloat16
I32 = mybir.dt.int32
U32 = mybir.dt.uint32
U16 = mybir.dt.uint16
U8 = mybir.dt.uint8
FP8X4 = mybir.dt.float8_e4m3fn_x4
FP4X4 = mybir.dt.float4_e2m1fn_x4
ALU = mybir.AluOpType
ACT = mybir.ActivationFunctionType

P = 128
PACK = 4
T = 2048
S = 512
HALF = S // 2
SLICES = ((0, 256), (256, 128), (384, 128))
FLOPS = 2 * 2 * 512 * 512 * 512


def tile_picked_skipgatebminmod_none_po_kernel(
    tc, x_words, x_scales, w1_words, w1_scales, gn, w2_words, w2_scales, offs, n1, n2, n3, n4, out_0, out_1, out_2
):
    nc = tc.nc
    with ExitStack() as ctx:
        lists = ctx.enter_context(tc.tile_pool(name="lists", bufs=1))
        keep = ctx.enter_context(tc.tile_pool(name="keep", bufs=1))
        psum = ctx.enter_context(tc.psum_pool(name="psum", bufs=1))

        def load_list(src, name):
            tile = lists.tile([P, S // 16], U16, name=name)
            nc.sync.dma_start(tile[:], src)
            return tile

        def load_scale_rows(tile, src, queues):
            for q, queue in queues.items():
                queue.dma_start(tile[32 * q : 32 * q + 4, :].bitcast(I32), src[0, 4 * q : 4 * q + 4, :].bitcast(I32))

        def deal_words(raw, name):
            words = keep.tile([P, PACK * P * 2], U8, name=name, align_bytes=64)
            nc.vector.tensor_copy(
                words[:].rearrange("p (t m b) -> p t m b", t=PACK, b=2),
                raw[:].rearrange("p (m t b) -> p t m b", t=PACK, b=2),
            )
            return words

        def deal_scales(raw, name):
            scales = keep.tile([P, PACK * P], U8, name=name, align_bytes=64)
            nc.vector.tensor_copy(
                scales[:].rearrange("p (t m) -> p t m", t=PACK),
                raw[:].rearrange("p (m t) -> p t m", t=PACK),
            )
            return scales

        def product(out, w_words, w_scales, t, codes, scales):
            nc.tensor.matmul_mx(
                out,
                lhsT=w_words[:, 2 * P * t : 2 * P * (t + 1)].bitcast(FP4X4),
                lhsT_scale=w_scales[:, P * t : P * (t + 1)],
                rhs=codes.bitcast(FP8X4),
                rhs_scale=scales,
                start=True,
                stop=True,
            )

        def picked(window, offsets, c0, width):
            return window[:].indirect(offsets[:, c0 // 16 : (c0 + width) // 16])

        def interleave(copy, dst, src):
            copy(dst.rearrange("p (c i) t -> p c t i", i=4), src.rearrange("p t (c i) -> p c t i", i=4))

        xs_raw = keep.tile([P, T], U8, name="xs_raw")
        w1s_raw = keep.tile([P, S], U8, name="w1s_raw")
        w2s_raw = keep.tile([P, S], U8, name="w2s_raw")
        nc.vector.memset(xs_raw[:].bitcast(I32), 0)
        nc.gpsimd.memset(w1s_raw[:].bitcast(I32), 0)
        nc.vector.memset(w2s_raw[:].bitcast(I32), 0)

        offs_t = load_list(offs, "offs_t")
        w1w_raw = keep.tile([P, 2 * S], U8, name="w1w_raw")
        nc.sync.dma_start(w1w_raw[:].bitcast(I32), w1_words[0].bitcast(I32))
        load_scale_rows(xs_raw, x_scales, {0: nc.scalar, 1: nc.sync, 2: nc.scalar, 3: nc.sync})
        load_scale_rows(w1s_raw, w1_scales, {0: nc.gpsimd, 1: nc.gpsimd, 2: nc.scalar})
        xw_raw = keep.tile([P, T], U32, name="xw_raw")
        nc.sync.dma_start(xw_raw[:].bitcast(I32), x_words[0].rearrange("p n t -> p (n t)").bitcast(I32))
        load_scale_rows(w1s_raw, w1_scales, {3: nc.sync})
        gain = keep.tile([P, PACK], F32, name="gain")
        nc.sync.dma_start(gain[:], gn.rearrange("(p t) o -> p (t o)", t=PACK))
        w2w_raw = keep.tile([P, 2 * S], U8, name="w2w_raw")
        nc.sync.dma_start(w2w_raw[:].bitcast(I32), w2_words[0].bitcast(I32))
        n1_t = load_list(n1, "n1_t")
        n2_t = load_list(n2, "n2_t")
        load_scale_rows(w2s_raw, w2_scales, {0: nc.sync, 1: nc.sync, 2: nc.gpsimd, 3: nc.gpsimd})
        n4_t = load_list(n4, "n4_t")
        n3_t = load_list(n3, "n3_t")

        neg_gain = keep.tile([P, PACK], F32, name="neg_gain")
        nc.scalar.activation(neg_gain[:], gain[:], ACT.Copy, scale=-1.0)

        w1_w = deal_words(w1w_raw, "w1_w")
        xs = keep.tile([P, S], U8, name="xs", align_bytes=64)
        nc.vector.tensor_copy(xs[:], xs_raw[:].indirect(offs_t[:]))

        pos = [keep.tile([P, S], F32, name=f"pos{t}") for t in range(PACK)]
        neg = [keep.tile([P, S], F32, name=f"neg{t}") for t in range(PACK)]
        y_sb = [keep.tile([P, S], F32, name=f"y{t}") for t in range(PACK)]
        half_h = [keep.tile([P, S], F32, name=f"half_h{t}") for t in range(PACK)]

        y_ps = {}
        for hf in range(2):
            xw = keep.tile([P, HALF], U32, name=f"xw{hf}", align_bytes=64)
            nc.vector.tensor_copy(xw[:], picked(xw_raw, offs_t, hf * HALF, HALF))
            if hf == 0:
                w1_s = deal_scales(w1s_raw, "w1_s")
            for t in range(PACK):
                bank = psum.tile([P, HALF], F32, name=f"y_bank{hf}{t}", tag=f"bank{hf}{t}")
                product(bank[:], w1_w, w1_s, t, xw[:], xs[:, hf * HALF : (hf + 1) * HALF])
                y_ps[hf, t] = bank[:]
        for t in range(PACK):
            for hf in range(2):
                cols = slice(hf * HALF, (hf + 1) * HALF)
                nc.scalar.activation(neg[t][:, cols], y_ps[hf, t], ACT.Copy, scale=neg_gain[:, t : t + 1])
                nc.scalar.activation(pos[t][:, cols], y_ps[hf, t], ACT.Copy, scale=gain[:, t : t + 1])
        w2_w = deal_words(w2w_raw, "w2_w")
        w2_s = deal_scales(w2s_raw, "w2_s")
        for t in range(PACK):
            for hf in range(2):
                nc.scalar.copy(y_sb[t][:, hf * HALF : (hf + 1) * HALF], y_ps[hf, t])

        def look_up_differences(hf):
            c0 = hf * HALF
            cols = slice(c0, c0 + HALF)
            pa = keep.tile([P, PACK, HALF], F32, name=f"pa{hf}", tag="pa", align_bytes=64)
            pb = keep.tile([P, PACK, HALF], F32, name=f"pb{hf}", tag="pb", align_bytes=64)
            for t in range(PACK):
                nc.vector.tensor_tensor(pa[:, t, :], picked(neg[t], n1_t, c0, HALF), pos[t][:, cols], ALU.add)
                nc.vector.tensor_tensor(pb[:, t, :], picked(pos[t], n2_t, c0, HALF), neg[t][:, cols], ALU.add)
            return pa, pb

        def minmod(hf, pa, pb, parts):
            floor = keep.tile([P, PACK, HALF], F32, name=f"floor{hf}", tag=f"staged{hf}", align_bytes=64)
            z = keep.tile([P, PACK, HALF], F32, name=f"z{hf}")
            for part in parts:
                nc.vector.scalar_tensor_tensor(floor[part], pb[part], 0.0, pa[part], ALU.min, ALU.max)
            for part in parts:
                nc.vector.scalar_tensor_tensor(z[part], pb[part], 0.0, floor[part], ALU.max, ALU.min)
            return z

        def look_up_gate(s):
            c0, width = SLICES[s]
            gate = keep.tile([P, PACK, width], F32, name=f"gate{s}")
            for t in range(PACK):
                nc.scalar.activation(gate[:, t, :], picked(y_sb[t], n4_t, c0, width), ACT.Sigmoid)
            return gate

        def round_z(s, z, copy, tag):
            c0, width = SLICES[s]
            z_bf = keep.tile([P, width, PACK], BF16, name=f"z_bf{s}", tag=tag, align_bytes=64)
            interleave(copy, z_bf[:], z[:, :, c0 % HALF : c0 % HALF + width])
            return z_bf

        def second_product(s, z_bf):
            c0, width = SLICES[s]
            z_codes = keep.tile([P, width], U32, name=f"z_codes{s}", align_bytes=64)
            z_scales = keep.tile([P, width], U8, name=f"z_scales{s}", align_bytes=64)
            nc.vector.quantize_mx(z_codes[:].bitcast(FP8X4), z_scales[:], z_bf[:].rearrange("p c t -> p (c t)"))
            per_bank = S // width
            banks = []
            for b in range(PACK // per_bank):
                bank = psum.tile([P, per_bank, width], F32, name=f"h_bank{s}{b}", tag=f"bank{min(s, 1)}{b + s // 2}")
                for u in range(per_bank):
                    product(bank[:, u, :], w2_w, w2_s, b * per_bank + u, z_codes[:], z_scales[:])
                for u in range(per_bank):
                    nc.scalar.activation(half_h[b * per_bank + u][:, c0 : c0 + width], bank[:, u, :], ACT.Copy, scale=-0.5)
                banks.append(bank)
            return banks

        every = slice(None)
        by_rows = [(every, slice(0, 2), every), (every, slice(2, 4), every)]
        by_cols = [(every, every, slice(0, HALF // 2)), (every, every, slice(HALF // 2, HALF))]

        pa, pb = look_up_differences(0)
        gates = [look_up_gate(0)]
        z = minmod(0, pa, pb, by_rows)
        z_bf = round_z(0, z, nc.scalar.copy, "staged1")
        pa, pb = look_up_differences(1)
        gates.append(look_up_gate(1))
        h_banks = [second_product(0, z_bf)]
        z = minmod(1, pa, pb, by_cols)
        z_bf1 = round_z(1, z, nc.scalar.copy, "z_bf1")
        z_bf2 = round_z(2, z, nc.vector.tensor_copy, "z_bf2")
        h_banks.append(second_product(1, z_bf1))
        h_banks.append(second_product(2, z_bf2))
        gates.append(look_up_gate(2))

        def gate_h(s, tag):
            c0, width = SLICES[s]
            gated_s = keep.tile([P, PACK, width], F32, name=f"gated{s}", tag=tag, align_bytes=64)
            per_bank = S // width
            for b, bank in enumerate(h_banks[s]):
                rows = slice(b * per_bank, (b + 1) * per_bank)
                nc.vector.tensor_tensor(gated_s[:, rows, :], bank[:], gates[s][:, rows, :], ALU.mult)
            return gated_s

        gated = [gate_h(0, "pb"), gate_h(1, "pa")]

        out_rows = out_0.rearrange("(p t) s -> p t s", t=PACK)
        out_words = out_1[0].rearrange("p n t -> p (n t)").bitcast(I32)
        o_scales = keep.tile([P, S], U8, name="o_scales", align_bytes=64)
        for s, (c0, width) in enumerate(SLICES):
            cols = slice(c0, c0 + width)
            last = s == len(SLICES) - 1
            res = keep.tile([P, PACK, width], F32, name=f"res{s}")
            for t in range(PACK):
                nc.vector.tensor_tensor(res[:, t, :], picked(half_h[t], n3_t, c0, width), gated[s][:, t, :], ALU.add)
            if s == 0:
                gated.append(gate_h(2, "gated2"))
            nc.sync.dma_start(out_rows[:, :, cols], res[:])
            o_bf = keep.tile([P, width, PACK], BF16, name=f"o_bf{s}", align_bytes=64)
            interleave(nc.vector.tensor_copy if last else nc.scalar.copy, o_bf[:], res[:])
            o_codes = keep.tile([P, width], U32, name=f"o_codes{s}", align_bytes=64)
            nc.vector.quantize_mx(o_codes[:].bitcast(FP8X4), o_scales[:, cols], o_bf[:].rearrange("p c t -> p (c t)"))
            nc.sync.dma_start(out_words[:, cols], o_codes[:].bitcast(I32))
        for q in range(4):
            queue = nc.scalar if q % 2 == 0 else nc.sync
            queue.dma_start(out_2[0, 4 * q : 4 * q + 4, :].bitcast(I32), o_scales[32 * q : 32 * q + 4, :].bitcast(I32))
